import numpy as np
import ml_dtypes


def mxq(x, axis, fmt="e4m3"):
    dtype, down = {"e4m3": (ml_dtypes.float8_e4m3fn, 7), "e5m2": (ml_dtypes.float8_e5m2, 14)}[fmt]
    v = np.moveaxis(np.asarray(x, np.float32).astype(ml_dtypes.bfloat16).astype(np.float64), axis, -1)
    blocks = v.reshape(v.shape[:-1] + (-1, 32))
    amax = np.abs(blocks).max(-1, keepdims=True)
    byte = np.maximum(np.where(amax > 0, np.frexp(amax)[1] - 1 + 127, 0) - down, 1)
    scale = np.exp2(byte - 127.0)
    codes = (blocks / scale).astype(np.float32).astype(dtype).astype(np.float64)
    return np.moveaxis((codes * scale).reshape(v.shape), -1, axis)


WIDE = False


def mx_kscale(k):
    if not WIDE:
        return np.ones(k)
    levels = np.array([10, -10, 5, -5, 0])
    if k % 512:
        return np.exp2(np.random.permutation(np.resize(levels, k // 32))).repeat(32)
    a = np.empty((k // 512, 16))
    for p in range(k // 512):
        a[p, :8] = np.random.permutation(np.resize(levels, 8))
        for g in range(8):
            far = levels[np.abs(levels - a[p, g]) >= 10]
            a[p, g + 8] = far[np.random.randint(len(far))]
    return np.exp2(a.ravel()).repeat(32)


def f64(x):
    return np.asarray(x).astype(np.float64)


def striped(idx):
    return np.tile(np.asarray(idx).reshape(-1, 16).T, (8, 1)).astype(np.uint16)


def unstriped(offs):
    return offs[:16].T.reshape(-1).astype(np.int64)


E2M1 = np.array([0.0, 0.5, 1.0, 1.5, 2.0, 3.0, 4.0, 6.0, -0.0, -0.5, -1.0, -1.5, -2.0, -3.0, -4.0, -6.0])


def pack_weight(w, fmt):
    k, n = w.shape
    w = f64(np.asarray(w, np.float32).astype(ml_dtypes.bfloat16)).reshape(k // 32, 32, n)
    amax = np.abs(w).max(1)
    if fmt == "e4m3":
        byte = np.frexp(amax)[1] - 1 + 127 - 7
    else:
        mant, ex = np.frexp(amax / 6.0)
        byte = np.where(mant > 0.5, ex, ex - 1) + 127
    byte = np.clip(np.where(amax > 0, byte, 1), 1, 254)
    scaled = (w * np.exp2(127.0 - byte)[:, None, :]).reshape(k, n).astype(np.float32)
    by_word = np.ascontiguousarray(scaled.reshape(k // 512, 128, 4, n).transpose(0, 1, 3, 2))
    if fmt == "e4m3":
        words = by_word.astype(ml_dtypes.float8_e4m3fn).view(np.uint8)
    else:
        c = by_word.astype(ml_dtypes.float4_e2m1fn).view(np.uint8) & 0xF
        words = (c[..., 0::2] | (c[..., 1::2] << 4)).reshape(k // 512, 128, 2 * n)
    return np.ascontiguousarray(words), np.ascontiguousarray(byte.astype(np.uint8).reshape(k // 512, 16, n))


def unpack_weight(words, scales, fmt):
    g, _, n = scales.shape
    words = np.ascontiguousarray(words).reshape(g, 128, n, -1)
    if fmt == "e4m3":
        vals = words.view(ml_dtypes.float8_e4m3fn).astype(np.float64)
    else:
        nib = np.empty((g, 128, n, 4), np.uint8)
        nib[..., 0::2] = words & 0xF
        nib[..., 1::2] = words >> 4
        vals = E2M1[nib]
    vals = vals * np.repeat(np.exp2(scales.astype(np.float64) - 127.0), 8, axis=1)[..., None]
    return vals.transpose(0, 1, 3, 2).reshape(g * 512, n)


C, T, I, D = 512, 2048, 512, 512


def setup_inputs():
    n = np.random.standard_normal
    idx = np.random.permutation(T)[:I]
    fc = mx_kscale(C)
    codep = pack_weight(n((C, T)) / fc[:, None], "e2m1")
    return {
        "code_words": codep[0],
        "code_scales": codep[1],
        "dec": (n((C, D)) * 1 / np.sqrt(C) * fc[:, None]).astype(np.float32),
        "keys": (n((D, T))).astype(np.float32),
        "offs": striped(idx),
    }


def reference(code_words, code_scales, dec, keys, offs):
    idx = unstriped(offs)
    codeu = unpack_weight(code_words, code_scales, "e2m1")
    decq = mxq(f64(dec), 0, "e4m3")
    codeidxg = codeu[:, idx]
    b = decq.T @ codeidxg
    y = f64(keys)[:, idx] - b
    return y

@@ -1,0 +1,99 @@
+from contextlib import ExitStack
+
+import concourse.mybir as mybir
+
+C, T, I, D = 512, 2048, 512, 512
+FLOPS = 2 * C * I * D
+
+F32 = mybir.dt.float32
+BF16 = mybir.dt.bfloat16
+I32 = mybir.dt.int32
+U32 = mybir.dt.uint32
+U16 = mybir.dt.uint16
+U8 = mybir.dt.uint8
+FP8X4 = mybir.dt.float8_e4m3fn_x4
+FP4X4 = mybir.dt.float4_e2m1fn_x4
+SUBTRACT = mybir.AluOpType.subtract
+
+P = 128
+PACK = 4
+BLOCKS = D // P
+HALF = D // 2
+LAST_PIECES = (256, 128, 128)
+
+
+def tile_attend_residualcache_kernel(tc, code_words, code_scales, dec, keys, offs, out):
+    nc = tc.nc
+    with ExitStack() as ctx:
+        keep = ctx.enter_context(tc.tile_pool(name="keep", bufs=1))
+        psum = ctx.enter_context(tc.psum_pool(name="psum", bufs=1))
+
+        scale_pool = keep.tile([P, T], U8, name="scale_pool", align_bytes=64)
+        nc.vector.memset(scale_pool[:].bitcast(I32), 0)
+
+        word_pool = keep.tile([P, T], U16, name="word_pool", align_bytes=64)
+        nc.sync.dma_start(word_pool[:].bitcast(I32), code_words[0].bitcast(I32))
+        offsets = keep.tile([P, I // 16], U16, name="offsets")
+        nc.sync.dma_start(offsets[:], offs)
+        for r in range(4):
+            nc.sync.dma_start(scale_pool[r:P:32, :].bitcast(I32), code_scales[0, r:16:4, :].bitcast(I32))
+        dec_raw = keep.tile([P, PACK, D], F32, name="dec_raw", align_bytes=64)
+        nc.sync.dma_start(dec_raw[:], dec.rearrange("(p j) d -> p j d", j=PACK))
+        key_pools = []
+        for b in range(BLOCKS):
+            key_pool = keep.tile([P, T], F32, name=f"key_pool{b}", align_bytes=64)
+            nc.sync.dma_start(key_pool[:], keys[b * P : (b + 1) * P, :])
+            key_pools.append(key_pool)
+
+        words = keep.tile([P, I], U16, name="words", align_bytes=64)
+        nc.vector.tensor_copy(words[:], word_pool[:].indirect(offsets[:]))
+        scales = keep.tile([P, I], U8, name="scales", align_bytes=64)
+        nc.vector.tensor_copy(scales[:], scale_pool[:].indirect(offsets[:]))
+
+        quantised = []
+        for h in range(2):
+            grouped = keep.tile([P, HALF, PACK], BF16, name=f"grouped{h}", align_bytes=64)
+            nc.scalar.copy(
+                grouped[:].rearrange("p (c i) j -> p c j i", i=4),
+                dec_raw[:, :, h * HALF : (h + 1) * HALF].rearrange("p j (c i) -> p c j i", i=4),
+            )
+            dec_codes = keep.tile([P, HALF], U32, name=f"dec_codes{h}", align_bytes=64)
+            dec_scales = keep.tile([P, HALF], U8, name=f"dec_scales{h}", align_bytes=64)
+            nc.vector.quantize_mx(
+                out=dec_codes[:].bitcast(FP8X4),
+                scales=dec_scales[:],
+                in_=grouped[:].rearrange("p d j -> p (d j)"),
+            )
+            quantised.append((dec_codes, dec_scales))
+
+        decoded = []
+        for b in range(BLOCKS):
+            dec_codes, dec_scales = quantised[b // 2]
+            cols = slice((b % 2) * P, (b % 2 + 1) * P)
+            bank = psum.tile([P, I], F32, name=f"bank{b}")
+            nc.tensor.matmul_mx(
+                out=bank[:],
+                lhsT=dec_codes[:, cols].bitcast(FP8X4),
+                lhsT_scale=dec_scales[:, cols],
+                rhs=words[:].bitcast(FP4X4),
+                rhs_scale=scales[:],
+                start=True,
+                stop=True,
+            )
+            sums = keep.tile([P, I], F32, name=f"sums{b}", align_bytes=64)
+            nc.scalar.copy(sums[:], bank[:])
+            decoded.append(sums)
+
+        for b in range(BLOCKS):
+            pieces = LAST_PIECES if b == BLOCKS - 1 else (I,)
+            first = 0
+            for n, width in enumerate(pieces):
+                residual = keep.tile([P, width], F32, name=f"residual{b}_{n}", align_bytes=64)
+                nc.vector.tensor_tensor(
+                    residual[:],
+                    key_pools[b][:].indirect(offsets[:, first // 16 : (first + width) // 16]),
+                    decoded[b][:, first : first + width],
+                    SUBTRACT,
+                )
+                nc.sync.dma_start(out[b * P : (b + 1) * P, first : first + width], residual[:])
+                first = first + width

@@ -53,10 +53,8 @@ def tile_attend_residualcache_kernel(tc, code_words, code_scales, dec, keys, off
         quantised = []
         for h in range(2):
             grouped = keep.tile([P, HALF, PACK], BF16, name=f"grouped{h}", align_bytes=64)
-            nc.scalar.copy(
-                grouped[:].rearrange("p (c i) j -> p c j i", i=4),
-                dec_raw[:, :, h * HALF : (h + 1) * HALF].rearrange("p j (c i) -> p c j i", i=4),
-            )
+            cast = nc.vector.tensor_copy if h == 0 else nc.scalar.copy
+            cast(grouped[:], dec_raw[:, :, h * HALF : (h + 1) * HALF].rearrange("p j d -> p d j"))
             dec_codes = keep.tile([P, HALF], U32, name=f"dec_codes{h}", align_bytes=64)
             dec_scales = keep.tile([P, HALF], U8, name=f"dec_scales{h}", align_bytes=64)
             nc.vector.quantize_mx(

@@ -18,7 +18,7 @@ SUBTRACT = mybir.AluOpType.subtract
 P = 128
 PACK = 4
 BLOCKS = D // P
-HALF = D // 2
+VECTOR_COLUMNS = 384
 LAST_PIECES = (256, 128, 128)
 
 
@@ -31,43 +31,42 @@ def tile_attend_residualcache_kernel(tc, code_words, code_scales, dec, keys, off
         scale_pool = keep.tile([P, T], U8, name="scale_pool", align_bytes=64)
         nc.vector.memset(scale_pool[:].bitcast(I32), 0)
 
-        word_pool = keep.tile([P, T], U16, name="word_pool", align_bytes=64)
-        nc.sync.dma_start(word_pool[:].bitcast(I32), code_words[0].bitcast(I32))
-        offsets = keep.tile([P, I // 16], U16, name="offsets")
-        nc.sync.dma_start(offsets[:], offs)
-        for r in range(4):
-            nc.sync.dma_start(scale_pool[r:P:32, :].bitcast(I32), code_scales[0, r:16:4, :].bitcast(I32))
         dec_raw = keep.tile([P, PACK, D], F32, name="dec_raw", align_bytes=64)
         nc.sync.dma_start(dec_raw[:], dec.rearrange("(p j) d -> p j d", j=PACK))
+        offsets = keep.tile([P, I // 16], U16, name="offsets")
+        nc.sync.dma_start(offsets[:], offs)
+        nc.sync.dma_start(scale_pool[0:P:8, :].bitcast(I32), code_scales[0].bitcast(I32))
+        word_pool = keep.tile([P, T], U16, name="word_pool", align_bytes=64)
+        nc.sync.dma_start(word_pool[:].bitcast(I32), code_words[0].bitcast(I32))
         key_pools = []
         for b in range(BLOCKS):
             key_pool = keep.tile([P, T], F32, name=f"key_pool{b}", align_bytes=64)
             nc.sync.dma_start(key_pool[:], keys[b * P : (b + 1) * P, :])
             key_pools.append(key_pool)
 
+        grouped = keep.tile([P, D, PACK], BF16, name="grouped", align_bytes=64)
+        by_column = dec_raw[:].rearrange("p j d -> p d j")
+        nc.vector.tensor_copy(grouped[:, :VECTOR_COLUMNS, :], by_column[:, :VECTOR_COLUMNS, :])
+        nc.scalar.copy(grouped[:, VECTOR_COLUMNS:, :], by_column[:, VECTOR_COLUMNS:, :])
+        dec_codes = keep.tile([P, D], U32, name="dec_codes", align_bytes=64)
+        dec_scales = keep.tile([P, D], U8, name="dec_scales", align_bytes=64)
+        nc.vector.quantize_mx(
+            out=dec_codes[:].bitcast(FP8X4),
+            scales=dec_scales[:],
+            in_=grouped[:].rearrange("p d j -> p (d j)"),
+        )
+
+        spread = keep.tile([P, I], U8, name="spread", align_bytes=64)
+        nc.vector.tensor_copy(spread[:], scale_pool[:].indirect(offsets[:]))
+        scales = keep.tile([P, I], U8, name="scales", align_bytes=64)
+        for r in range(4):
+            nc.scalar.dma_start(scales[r:P:32, :].bitcast(I32), spread[8 * r : P : 32, :].bitcast(I32))
         words = keep.tile([P, I], U16, name="words", align_bytes=64)
         nc.vector.tensor_copy(words[:], word_pool[:].indirect(offsets[:]))
-        scales = keep.tile([P, I], U8, name="scales", align_bytes=64)
-        nc.vector.tensor_copy(scales[:], scale_pool[:].indirect(offsets[:]))
-
-        quantised = []
-        for h in range(2):
-            grouped = keep.tile([P, HALF, PACK], BF16, name=f"grouped{h}", align_bytes=64)
-            cast = nc.vector.tensor_copy if h == 0 else nc.scalar.copy
-            cast(grouped[:], dec_raw[:, :, h * HALF : (h + 1) * HALF].rearrange("p j d -> p d j"))
-            dec_codes = keep.tile([P, HALF], U32, name=f"dec_codes{h}", align_bytes=64)
-            dec_scales = keep.tile([P, HALF], U8, name=f"dec_scales{h}", align_bytes=64)
-            nc.vector.quantize_mx(
-                out=dec_codes[:].bitcast(FP8X4),
-                scales=dec_scales[:],
-                in_=grouped[:].rearrange("p d j -> p (d j)"),
-            )
-            quantised.append((dec_codes, dec_scales))
 
         decoded = []
         for b in range(BLOCKS):
-            dec_codes, dec_scales = quantised[b // 2]
-            cols = slice((b % 2) * P, (b % 2 + 1) * P)
+            cols = slice(b * P, (b + 1) * P)
             bank = psum.tile([P, I], F32, name=f"bank{b}")
             nc.tensor.matmul_mx(
                 out=bank[:],

@@ -19,6 +19,7 @@ P = 128
 PACK = 4
 BLOCKS = D // P
 VECTOR_COLUMNS = 384
+EARLY = 2
 LAST_PIECES = (256, 128, 128)
 
 
@@ -28,7 +29,7 @@ def tile_attend_residualcache_kernel(tc, code_words, code_scales, dec, keys, off
         keep = ctx.enter_context(tc.tile_pool(name="keep", bufs=1))
         psum = ctx.enter_context(tc.psum_pool(name="psum", bufs=1))
 
-        scale_pool = keep.tile([P, T], U8, name="scale_pool", align_bytes=64)
+        scale_pool = keep.tile([P, T], U8, name="scale_pool", tag="after_scales", align_bytes=64)
         nc.vector.memset(scale_pool[:].bitcast(I32), 0)
 
         dec_raw = keep.tile([P, PACK, D], F32, name="dec_raw", align_bytes=64)
@@ -36,10 +37,10 @@ def tile_attend_residualcache_kernel(tc, code_words, code_scales, dec, keys, off
         offsets = keep.tile([P, I // 16], U16, name="offsets")
         nc.sync.dma_start(offsets[:], offs)
         nc.sync.dma_start(scale_pool[0:P:8, :].bitcast(I32), code_scales[0].bitcast(I32))
-        word_pool = keep.tile([P, T], U16, name="word_pool", align_bytes=64)
+        word_pool = keep.tile([P, T], U16, name="word_pool", tag="after_words", align_bytes=64)
         nc.sync.dma_start(word_pool[:].bitcast(I32), code_words[0].bitcast(I32))
         key_pools = []
-        for b in range(BLOCKS):
+        for b in range(EARLY):
             key_pool = keep.tile([P, T], F32, name=f"key_pool{b}", align_bytes=64)
             nc.sync.dma_start(key_pool[:], keys[b * P : (b + 1) * P, :])
             key_pools.append(key_pool)
@@ -60,12 +61,23 @@ def tile_attend_residualcache_kernel(tc, code_words, code_scales, dec, keys, off
         nc.vector.tensor_copy(spread[:], scale_pool[:].indirect(offsets[:]))
         scales = keep.tile([P, I], U8, name="scales", align_bytes=64)
         for r in range(4):
-            nc.scalar.dma_start(scales[r:P:32, :].bitcast(I32), spread[8 * r : P : 32, :].bitcast(I32))
+            nc.sync.dma_start(scales[r:P:32, :].bitcast(I32), spread[8 * r : P : 32, :].bitcast(I32))
         words = keep.tile([P, I], U16, name="words", align_bytes=64)
         nc.vector.tensor_copy(words[:], word_pool[:].indirect(offsets[:]))
 
-        decoded = []
-        for b in range(BLOCKS):
+        for b, tag in ((2, "after_scales"), (3, "after_words")):
+            key_pool = keep.tile([P, T], F32, name=f"key_pool{b}", tag=tag, align_bytes=64)
+            nc.sync.dma_start(key_pool[:], keys[b * P : (b + 1) * P, :])
+            key_pools.append(key_pool)
+
+        listed = []
+        for b in range(EARLY):
+            listed_keys = keep.tile([P, I], F32, name=f"listed_keys{b}", align_bytes=64)
+            nc.vector.tensor_copy(listed_keys[:], key_pools[b][:].indirect(offsets[:]))
+            listed.append(listed_keys)
+
+        decoded = {}
+        for b in (2, 0, 1, 3):
             cols = slice(b * P, (b + 1) * P)
             bank = psum.tile([P, I], F32, name=f"bank{b}")
             nc.tensor.matmul_mx(
@@ -77,11 +89,19 @@ def tile_attend_residualcache_kernel(tc, code_words, code_scales, dec, keys, off
                 start=True,
                 stop=True,
             )
-            sums = keep.tile([P, I], F32, name=f"sums{b}", align_bytes=64)
-            nc.scalar.copy(sums[:], bank[:])
-            decoded.append(sums)
+            if b < EARLY:
+                decoded[b] = bank
+            else:
+                sums = keep.tile([P, I], F32, name=f"sums{b}", align_bytes=64)
+                nc.scalar.copy(sums[:], bank[:])
+                decoded[b] = sums
 
-        for b in range(BLOCKS):
+        for b in range(EARLY):
+            residual = keep.tile([P, I], F32, name=f"residual{b}", align_bytes=64)
+            nc.vector.tensor_tensor(residual[:], listed[b][:], decoded[b][:], SUBTRACT)
+            nc.sync.dma_start(out[b * P : (b + 1) * P, :], residual[:])
+
+        for b in range(EARLY, BLOCKS):
             pieces = LAST_PIECES if b == BLOCKS - 1 else (I,)
             first = 0
             for n, width in enumerate(pieces):

@@ -20,7 +20,7 @@ PACK = 4
 BLOCKS = D // P
 VECTOR_COLUMNS = 384
 EARLY = 2
-LAST_PIECES = (256, 128, 128)
+LAST_PIECES = (384, 128)
 
 
 def tile_attend_residualcache_kernel(tc, code_words, code_scales, dec, keys, offs, out):

@@ -36,7 +36,7 @@ def tile_attend_residualcache_kernel(tc, code_words, code_scales, dec, keys, off
         nc.sync.dma_start(dec_raw[:], dec.rearrange("(p j) d -> p j d", j=PACK))
         offsets = keep.tile([P, I // 16], U16, name="offsets")
         nc.sync.dma_start(offsets[:], offs)
-        nc.sync.dma_start(scale_pool[0:P:8, :].bitcast(I32), code_scales[0].bitcast(I32))
+        nc.sync.dma_start(scale_pool[32:96:4, :].bitcast(I32), code_scales[0].bitcast(I32))
         word_pool = keep.tile([P, T], U16, name="word_pool", tag="after_words", align_bytes=64)
         nc.sync.dma_start(word_pool[:].bitcast(I32), code_words[0].bitcast(I32))
         key_pools = []
@@ -61,7 +61,7 @@ def tile_attend_residualcache_kernel(tc, code_words, code_scales, dec, keys, off
         nc.vector.tensor_copy(spread[:], scale_pool[:].indirect(offsets[:]))
         scales = keep.tile([P, I], U8, name="scales", align_bytes=64)
         for r in range(4):
-            nc.sync.dma_start(scales[r:P:32, :].bitcast(I32), spread[8 * r : P : 32, :].bitcast(I32))
+            nc.sync.dma_start(scales[r:P:32, :].bitcast(I32), spread[32 + 4 * r : 96 : 16, :].bitcast(I32))
         words = keep.tile([P, I], U16, name="words", align_bytes=64)
         nc.vector.tensor_copy(words[:], word_pool[:].indirect(offsets[:]))
 
@@ -96,10 +96,10 @@ def tile_attend_residualcache_kernel(tc, code_words, code_scales, dec, keys, off
                 nc.scalar.copy(sums[:], bank[:])
                 decoded[b] = sums
 
+        early_residual = keep.tile([P, EARLY, I], F32, name="early_residual", align_bytes=64)
         for b in range(EARLY):
-            residual = keep.tile([P, I], F32, name=f"residual{b}", align_bytes=64)
-            nc.vector.tensor_tensor(residual[:], listed[b][:], decoded[b][:], SUBTRACT)
-            nc.sync.dma_start(out[b * P : (b + 1) * P, :], residual[:])
+            nc.vector.tensor_tensor(early_residual[:, b, :], listed[b][:], decoded[b][:], SUBTRACT)
+        nc.sync.dma_start(out[: EARLY * P, :].rearrange("(b p) i -> p b i", p=P), early_residual[:])
 
         for b in range(EARLY, BLOCKS):
             pieces = LAST_PIECES if b == BLOCKS - 1 else (I,)

@@ -20,7 +20,7 @@ PACK = 4
 BLOCKS = D // P
 VECTOR_COLUMNS = 384
 EARLY = 2
-LAST_PIECES = (384, 128)
+LAST_PIECES = (320, 192)
 
 
 def tile_attend_residualcache_kernel(tc, code_words, code_scales, dec, keys, offs, out):
@@ -77,24 +77,28 @@ def tile_attend_residualcache_kernel(tc, code_words, code_scales, dec, keys, off
             listed.append(listed_keys)
 
         decoded = {}
-        for b in (2, 0, 1, 3):
+        for b in range(BLOCKS):
             cols = slice(b * P, (b + 1) * P)
-            bank = psum.tile([P, I], F32, name=f"bank{b}")
-            nc.tensor.matmul_mx(
-                out=bank[:],
-                lhsT=dec_codes[:, cols].bitcast(FP8X4),
-                lhsT_scale=dec_scales[:, cols],
-                rhs=words[:].bitcast(FP4X4),
-                rhs_scale=scales[:],
-                start=True,
-                stop=True,
-            )
-            if b < EARLY:
-                decoded[b] = bank
-            else:
-                sums = keep.tile([P, I], F32, name=f"sums{b}", align_bytes=64)
-                nc.scalar.copy(sums[:], bank[:])
-                decoded[b] = sums
+            halves = 2 if b == EARLY else 1
+            width = I // halves
+            if b >= EARLY:
+                decoded[b] = keep.tile([P, I], F32, name=f"sums{b}", align_bytes=64)
+            for h in range(halves):
+                slots = slice(h * width, (h + 1) * width)
+                bank = psum.tile([P, width], F32, name=f"bank{b}_{h}")
+                nc.tensor.matmul_mx(
+                    out=bank[:],
+                    lhsT=dec_codes[:, cols].bitcast(FP8X4),
+                    lhsT_scale=dec_scales[:, cols],
+                    rhs=words[:, slots].bitcast(FP4X4),
+                    rhs_scale=scales[:, slots],
+                    start=True,
+                    stop=True,
+                )
+                if b < EARLY:
+                    decoded[b] = bank
+                else:
+                    nc.scalar.copy(decoded[b][:, slots], bank[:])
 
         early_residual = keep.tile([P, EARLY, I], F32, name="early_residual", align_bytes=64)
         for b in range(EARLY):

@@ -20,7 +20,7 @@ PACK = 4
 BLOCKS = D // P
 VECTOR_COLUMNS = 384
 EARLY = 2
-LAST_PIECES = (320, 192)
+LAST_PIECES = (288, 160, 64)
 
 
 def tile_attend_residualcache_kernel(tc, code_words, code_scales, dec, keys, offs, out):
@@ -36,7 +36,7 @@ def tile_attend_residualcache_kernel(tc, code_words, code_scales, dec, keys, off
         nc.sync.dma_start(dec_raw[:], dec.rearrange("(p j) d -> p j d", j=PACK))
         offsets = keep.tile([P, I // 16], U16, name="offsets")
         nc.sync.dma_start(offsets[:], offs)
-        nc.sync.dma_start(scale_pool[32:96:4, :].bitcast(I32), code_scales[0].bitcast(I32))
+        nc.sync.dma_start(scale_pool[0:P:8, :].bitcast(I32), code_scales[0].bitcast(I32))
         word_pool = keep.tile([P, T], U16, name="word_pool", tag="after_words", align_bytes=64)
         nc.sync.dma_start(word_pool[:].bitcast(I32), code_words[0].bitcast(I32))
         key_pools = []
@@ -60,8 +60,9 @@ def tile_attend_residualcache_kernel(tc, code_words, code_scales, dec, keys, off
         spread = keep.tile([P, I], U8, name="spread", align_bytes=64)
         nc.vector.tensor_copy(spread[:], scale_pool[:].indirect(offsets[:]))
         scales = keep.tile([P, I], U8, name="scales", align_bytes=64)
-        for r in range(4):
-            nc.sync.dma_start(scales[r:P:32, :].bitcast(I32), spread[32 + 4 * r : 96 : 16, :].bitcast(I32))
+        nc.vector.tensor_copy(scales[:].bitcast(I32), spread[:].bitcast(I32))
+        for r in range(1, 4):
+            nc.sync.dma_start(scales[r:P:32, :].bitcast(I32), spread[8 * r : P : 32, :].bitcast(I32))
         words = keep.tile([P, I], U16, name="words", align_bytes=64)
         nc.vector.tensor_copy(words[:], word_pool[:].indirect(offsets[:]))
 

@@ -18,7 +18,7 @@ SUBTRACT = mybir.AluOpType.subtract
 P = 128
 PACK = 4
 BLOCKS = D // P
-VECTOR_COLUMNS = 384
+VECTOR_COLUMNS = 256
 EARLY = 2
 LAST_PIECES = (288, 160, 64)
 
@@ -27,9 +27,10 @@ def tile_attend_residualcache_kernel(tc, code_words, code_scales, dec, keys, off
     nc = tc.nc
     with ExitStack() as ctx:
         keep = ctx.enter_context(tc.tile_pool(name="keep", bufs=1))
+        shared = ctx.enter_context(tc.tile_pool(name="shared", bufs=1))
         psum = ctx.enter_context(tc.psum_pool(name="psum", bufs=1))
 
-        scale_pool = keep.tile([P, T], U8, name="scale_pool", tag="after_scales", align_bytes=64)
+        scale_pool = shared.tile([P, T], U8, name="scale_pool", align_bytes=64, offset=4 * T - T // 4)
         nc.vector.memset(scale_pool[:].bitcast(I32), 0)
 
         dec_raw = keep.tile([P, PACK, D], F32, name="dec_raw", align_bytes=64)
@@ -49,13 +50,6 @@ def tile_attend_residualcache_kernel(tc, code_words, code_scales, dec, keys, off
         by_column = dec_raw[:].rearrange("p j d -> p d j")
         nc.vector.tensor_copy(grouped[:, :VECTOR_COLUMNS, :], by_column[:, :VECTOR_COLUMNS, :])
         nc.scalar.copy(grouped[:, VECTOR_COLUMNS:, :], by_column[:, VECTOR_COLUMNS:, :])
-        dec_codes = keep.tile([P, D], U32, name="dec_codes", align_bytes=64)
-        dec_scales = keep.tile([P, D], U8, name="dec_scales", align_bytes=64)
-        nc.vector.quantize_mx(
-            out=dec_codes[:].bitcast(FP8X4),
-            scales=dec_scales[:],
-            in_=grouped[:].rearrange("p d j -> p (d j)"),
-        )
 
         spread = keep.tile([P, I], U8, name="spread", align_bytes=64)
         nc.vector.tensor_copy(spread[:], scale_pool[:].indirect(offsets[:]))
@@ -63,13 +57,21 @@ def tile_attend_residualcache_kernel(tc, code_words, code_scales, dec, keys, off
         nc.vector.tensor_copy(scales[:].bitcast(I32), spread[:].bitcast(I32))
         for r in range(1, 4):
             nc.sync.dma_start(scales[r:P:32, :].bitcast(I32), spread[8 * r : P : 32, :].bitcast(I32))
-        words = keep.tile([P, I], U16, name="words", align_bytes=64)
+        dec_codes = shared.tile([P, D], U32, name="dec_codes", align_bytes=64, offset=4 * T + 2 * I)
+        dec_scales = keep.tile([P, D], U8, name="dec_scales", align_bytes=64)
+        nc.vector.quantize_mx(
+            out=dec_codes[:].bitcast(FP8X4),
+            scales=dec_scales[:],
+            in_=grouped[:].rearrange("p d j -> p (d j)"),
+        )
+
+        words = shared.tile([P, I], U16, name="words", align_bytes=64, offset=4 * T)
         nc.vector.tensor_copy(words[:], word_pool[:].indirect(offsets[:]))
 
-        for b, tag in ((2, "after_scales"), (3, "after_words")):
-            key_pool = keep.tile([P, T], F32, name=f"key_pool{b}", tag=tag, align_bytes=64)
-            nc.sync.dma_start(key_pool[:], keys[b * P : (b + 1) * P, :])
-            key_pools.append(key_pool)
+        key_pools.append(shared.tile([P, T], F32, name="key_pool2", align_bytes=64, offset=0))
+        key_pools.append(keep.tile([P, T], F32, name="key_pool3", tag="after_words", align_bytes=64))
+        for b in range(EARLY, BLOCKS):
+            nc.sync.dma_start(key_pools[b][:], keys[b * P : (b + 1) * P, :])
 
         listed = []
         for b in range(EARLY):

@@ -18,7 +18,6 @@ SUBTRACT = mybir.AluOpType.subtract
 P = 128
 PACK = 4
 BLOCKS = D // P
-VECTOR_COLUMNS = 256
 EARLY = 2
 LAST_PIECES = (288, 160, 64)
 
@@ -43,13 +42,16 @@ def tile_attend_residualcache_kernel(tc, code_words, code_scales, dec, keys, off
         key_pools = []
         for b in range(EARLY):
             key_pool = keep.tile([P, T], F32, name=f"key_pool{b}", align_bytes=64)
-            nc.sync.dma_start(key_pool[:], keys[b * P : (b + 1) * P, :])
+            nc.sync.dma_start(key_pool[:], keys[b : EARLY * P : EARLY, :])
             key_pools.append(key_pool)
 
         grouped = keep.tile([P, D, PACK], BF16, name="grouped", align_bytes=64)
         by_column = dec_raw[:].rearrange("p j d -> p d j")
-        nc.vector.tensor_copy(grouped[:, :VECTOR_COLUMNS, :], by_column[:, :VECTOR_COLUMNS, :])
-        nc.scalar.copy(grouped[:, VECTOR_COLUMNS:, :], by_column[:, VECTOR_COLUMNS:, :])
+        nc.scalar.copy(
+            grouped[:, : EARLY * P, :].rearrange("p (b m) j -> p m b j", b=EARLY),
+            by_column[:, : EARLY * P, :].rearrange("p (m b) j -> p m b j", b=EARLY),
+        )
+        nc.vector.tensor_copy(grouped[:, EARLY * P :, :], by_column[:, EARLY * P :, :])
 
         spread = keep.tile([P, I], U8, name="spread", align_bytes=64)
         nc.vector.tensor_copy(spread[:], scale_pool[:].indirect(offsets[:]))
@@ -106,7 +108,7 @@ def tile_attend_residualcache_kernel(tc, code_words, code_scales, dec, keys, off
         early_residual = keep.tile([P, EARLY, I], F32, name="early_residual", align_bytes=64)
         for b in range(EARLY):
             nc.vector.tensor_tensor(early_residual[:, b, :], listed[b][:], decoded[b][:], SUBTRACT)
-        nc.sync.dma_start(out[: EARLY * P, :].rearrange("(b p) i -> p b i", p=P), early_residual[:])
+        nc.sync.dma_start(out[: EARLY * P, :].rearrange("(p b) i -> p b i", b=EARLY), early_residual[:])
 
         for b in range(EARLY, BLOCKS):
             pieces = LAST_PIECES if b == BLOCKS - 1 else (I,)

@@ -19,7 +19,7 @@ P = 128
 PACK = 4
 BLOCKS = D // P
 EARLY = 2
-LAST_PIECES = (288, 160, 64)
+LAST_PIECES = (256, 192, 64)
 
 
 def tile_attend_residualcache_kernel(tc, code_words, code_scales, dec, keys, offs, out):
@@ -29,23 +29,23 @@ def tile_attend_residualcache_kernel(tc, code_words, code_scales, dec, keys, off
         shared = ctx.enter_context(tc.tile_pool(name="shared", bufs=1))
         psum = ctx.enter_context(tc.psum_pool(name="psum", bufs=1))
 
-        scale_pool = shared.tile([P, T], U8, name="scale_pool", align_bytes=64, offset=4 * T - T // 4)
+        scale_pool = shared.tile([P, T], U8, name="scale_pool", align_bytes=256, offset=4 * T - T // 4)
         nc.vector.memset(scale_pool[:].bitcast(I32), 0)
 
-        dec_raw = keep.tile([P, PACK, D], F32, name="dec_raw", align_bytes=64)
+        dec_raw = keep.tile([P, PACK, D], F32, name="dec_raw", align_bytes=256)
         nc.sync.dma_start(dec_raw[:], dec.rearrange("(p j) d -> p j d", j=PACK))
-        offsets = keep.tile([P, I // 16], U16, name="offsets")
+        offsets = keep.tile([P, I // 16], U16, name="offsets", align_bytes=256)
         nc.sync.dma_start(offsets[:], offs)
         nc.sync.dma_start(scale_pool[0:P:8, :].bitcast(I32), code_scales[0].bitcast(I32))
-        word_pool = keep.tile([P, T], U16, name="word_pool", tag="after_words", align_bytes=64)
+        word_pool = keep.tile([P, T], U16, name="word_pool", tag="after_words", align_bytes=256)
         nc.sync.dma_start(word_pool[:].bitcast(I32), code_words[0].bitcast(I32))
         key_pools = []
         for b in range(EARLY):
-            key_pool = keep.tile([P, T], F32, name=f"key_pool{b}", align_bytes=64)
+            key_pool = keep.tile([P, T], F32, name=f"key_pool{b}", align_bytes=256)
             nc.sync.dma_start(key_pool[:], keys[b : EARLY * P : EARLY, :])
             key_pools.append(key_pool)
 
-        grouped = keep.tile([P, D, PACK], BF16, name="grouped", align_bytes=64)
+        grouped = keep.tile([P, D, PACK], BF16, name="grouped", align_bytes=256)
         by_column = dec_raw[:].rearrange("p j d -> p d j")
         nc.scalar.copy(
             grouped[:, : EARLY * P, :].rearrange("p (b m) j -> p m b j", b=EARLY),
@@ -53,31 +53,31 @@ def tile_attend_residualcache_kernel(tc, code_words, code_scales, dec, keys, off
         )
         nc.vector.tensor_copy(grouped[:, EARLY * P :, :], by_column[:, EARLY * P :, :])
 
-        spread = keep.tile([P, I], U8, name="spread", align_bytes=64)
+        spread = keep.tile([P, I], U8, name="spread", align_bytes=256)
         nc.vector.tensor_copy(spread[:], scale_pool[:].indirect(offsets[:]))
-        scales = keep.tile([P, I], U8, name="scales", align_bytes=64)
+        scales = keep.tile([P, I], U8, name="scales", align_bytes=256)
         nc.vector.tensor_copy(scales[:].bitcast(I32), spread[:].bitcast(I32))
         for r in range(1, 4):
             nc.sync.dma_start(scales[r:P:32, :].bitcast(I32), spread[8 * r : P : 32, :].bitcast(I32))
-        dec_codes = shared.tile([P, D], U32, name="dec_codes", align_bytes=64, offset=4 * T + 2 * I)
-        dec_scales = keep.tile([P, D], U8, name="dec_scales", align_bytes=64)
+        dec_codes = shared.tile([P, D], U32, name="dec_codes", align_bytes=256, offset=4 * T + 2 * I)
+        dec_scales = keep.tile([P, D], U8, name="dec_scales", align_bytes=256)
         nc.vector.quantize_mx(
             out=dec_codes[:].bitcast(FP8X4),
             scales=dec_scales[:],
             in_=grouped[:].rearrange("p d j -> p (d j)"),
         )
 
-        words = shared.tile([P, I], U16, name="words", align_bytes=64, offset=4 * T)
+        words = shared.tile([P, I], U16, name="words", align_bytes=256, offset=4 * T)
         nc.vector.tensor_copy(words[:], word_pool[:].indirect(offsets[:]))
 
-        key_pools.append(shared.tile([P, T], F32, name="key_pool2", align_bytes=64, offset=0))
-        key_pools.append(keep.tile([P, T], F32, name="key_pool3", tag="after_words", align_bytes=64))
+        key_pools.append(shared.tile([P, T], F32, name="key_pool2", align_bytes=256, offset=0))
+        key_pools.append(keep.tile([P, T], F32, name="key_pool3", tag="after_words", align_bytes=256))
         for b in range(EARLY, BLOCKS):
             nc.sync.dma_start(key_pools[b][:], keys[b * P : (b + 1) * P, :])
 
         listed = []
         for b in range(EARLY):
-            listed_keys = keep.tile([P, I], F32, name=f"listed_keys{b}", align_bytes=64)
+            listed_keys = keep.tile([P, I], F32, name=f"listed_keys{b}", align_bytes=256)
             nc.vector.tensor_copy(listed_keys[:], key_pools[b][:].indirect(offsets[:]))
             listed.append(listed_keys)
 
@@ -87,7 +87,7 @@ def tile_attend_residualcache_kernel(tc, code_words, code_scales, dec, keys, off
             halves = 2 if b == EARLY else 1
             width = I // halves
             if b >= EARLY:
-                decoded[b] = keep.tile([P, I], F32, name=f"sums{b}", align_bytes=64)
+                decoded[b] = keep.tile([P, I], F32, name=f"sums{b}", align_bytes=256)
             for h in range(halves):
                 slots = slice(h * width, (h + 1) * width)
                 bank = psum.tile([P, width], F32, name=f"bank{b}_{h}")
@@ -105,7 +105,7 @@ def tile_attend_residualcache_kernel(tc, code_words, code_scales, dec, keys, off
                 else:
                     nc.scalar.copy(decoded[b][:, slots], bank[:])
 
-        early_residual = keep.tile([P, EARLY, I], F32, name="early_residual", align_bytes=64)
+        early_residual = keep.tile([P, EARLY, I], F32, name="early_residual", align_bytes=256)
         for b in range(EARLY):
             nc.vector.tensor_tensor(early_residual[:, b, :], listed[b][:], decoded[b][:], SUBTRACT)
         nc.sync.dma_start(out[: EARLY * P, :].rearrange("(p b) i -> p b i", b=EARLY), early_residual[:])
@@ -114,7 +114,7 @@ def tile_attend_residualcache_kernel(tc, code_words, code_scales, dec, keys, off
             pieces = LAST_PIECES if b == BLOCKS - 1 else (I,)
             first = 0
             for n, width in enumerate(pieces):
-                residual = keep.tile([P, width], F32, name=f"residual{b}_{n}", align_bytes=64)
+                residual = keep.tile([P, width], F32, name=f"residual{b}_{n}", align_bytes=256)
                 nc.vector.tensor_tensor(
                     residual[:],
                     key_pools[b][:].indirect(offsets[:, first // 16 : (first + width) // 16]),

@@ -81,45 +81,51 @@ def tile_attend_residualcache_kernel(tc, code_words, code_scales, dec, keys, off
             nc.vector.tensor_copy(listed_keys[:], key_pools[b][:].indirect(offsets[:]))
             listed.append(listed_keys)
 
-        decoded = {}
-        for b in range(BLOCKS):
+        half = I // 2
+        sums = {b: keep.tile([P, I], F32, name=f"sums{b}", align_bytes=256) for b in range(EARLY, BLOCKS)}
+        passes = [(b, 0, I) for b in range(EARLY)] + [(EARLY, 0, half), (BLOCKS - 1, 0, I), (EARLY, half, I)]
+        decoded = dict(sums)
+        for b, lo, hi in passes:
             cols = slice(b * P, (b + 1) * P)
-            halves = 2 if b == EARLY else 1
-            width = I // halves
-            if b >= EARLY:
-                decoded[b] = keep.tile([P, I], F32, name=f"sums{b}", align_bytes=256)
-            for h in range(halves):
-                slots = slice(h * width, (h + 1) * width)
-                bank = psum.tile([P, width], F32, name=f"bank{b}_{h}")
-                nc.tensor.matmul_mx(
-                    out=bank[:],
-                    lhsT=dec_codes[:, cols].bitcast(FP8X4),
-                    lhsT_scale=dec_scales[:, cols],
-                    rhs=words[:, slots].bitcast(FP4X4),
-                    rhs_scale=scales[:, slots],
-                    start=True,
-                    stop=True,
-                )
-                if b < EARLY:
-                    decoded[b] = bank
-                else:
-                    nc.scalar.copy(decoded[b][:, slots], bank[:])
+            bank = psum.tile([P, hi - lo], F32, name=f"bank{b}_{lo}")
+            nc.tensor.matmul_mx(
+                out=bank[:],
+                lhsT=dec_codes[:, cols].bitcast(FP8X4),
+                lhsT_scale=dec_scales[:, cols],
+                rhs=words[:, lo:hi].bitcast(FP4X4),
+                rhs_scale=scales[:, lo:hi],
+                start=True,
+                stop=True,
+            )
+            if b < EARLY:
+                decoded[b] = bank
+            else:
+                nc.scalar.copy(sums[b][:, lo:hi], bank[:])
 
         early_residual = keep.tile([P, EARLY, I], F32, name="early_residual", align_bytes=256)
         for b in range(EARLY):
             nc.vector.tensor_tensor(early_residual[:, b, :], listed[b][:], decoded[b][:], SUBTRACT)
         nc.sync.dma_start(out[: EARLY * P, :].rearrange("(p b) i -> p b i", b=EARLY), early_residual[:])
 
-        for b in range(EARLY, BLOCKS):
-            pieces = LAST_PIECES if b == BLOCKS - 1 else (I,)
-            first = 0
-            for n, width in enumerate(pieces):
-                residual = keep.tile([P, width], F32, name=f"residual{b}_{n}", align_bytes=256)
-                nc.vector.tensor_tensor(
-                    residual[:],
-                    key_pools[b][:].indirect(offsets[:, first // 16 : (first + width) // 16]),
-                    decoded[b][:, first : first + width],
-                    SUBTRACT,
-                )
-                nc.sync.dma_start(out[b * P : (b + 1) * P, first : first + width], residual[:])
-                first = first + width
+        residual = keep.tile([P, I], F32, name="residual", align_bytes=256)
+        for lo in range(0, I, half):
+            nc.vector.tensor_tensor(
+                residual[:, lo : lo + half],
+                key_pools[EARLY][:].indirect(offsets[:, lo // 16 : (lo + half) // 16]),
+                decoded[EARLY][:, lo : lo + half],
+                SUBTRACT,
+            )
+        nc.sync.dma_start(out[EARLY * P : (EARLY + 1) * P, :], residual[:])
+
+        b = BLOCKS - 1
+        first = 0
+        for n, width in enumerate(LAST_PIECES):
+            piece = keep.tile([P, width], F32, name=f"piece{n}", align_bytes=256)
+            nc.vector.tensor_tensor(
+                piece[:],
+                key_pools[b][:].indirect(offsets[:, first // 16 : (first + width) // 16]),
+                decoded[b][:, first : first + width],
+                SUBTRACT,
+            )
+            nc.sync.dma_start(out[b * P : (b + 1) * P, first : first + width], piece[:])
+            first = first + width

@@ -29,19 +29,19 @@ def tile_attend_residualcache_kernel(tc, code_words, code_scales, dec, keys, off
         shared = ctx.enter_context(tc.tile_pool(name="shared", bufs=1))
         psum = ctx.enter_context(tc.psum_pool(name="psum", bufs=1))
 
-        scale_pool = shared.tile([P, T], U8, name="scale_pool", align_bytes=256, offset=4 * T - T // 4)
+        scale_pool = shared.tile([P, T], U8, name="scale_pool", align_bytes=512, offset=4 * T - T // 4)
         nc.vector.memset(scale_pool[:].bitcast(I32), 0)
 
-        dec_raw = keep.tile([P, PACK, D], F32, name="dec_raw", align_bytes=256)
+        dec_raw = keep.tile([P, PACK, D], F32, name="dec_raw", align_bytes=4096)
         nc.sync.dma_start(dec_raw[:], dec.rearrange("(p j) d -> p j d", j=PACK))
-        offsets = keep.tile([P, I // 16], U16, name="offsets", align_bytes=256)
+        offsets = keep.tile([P, I // 16], U16, name="offsets", align_bytes=512)
         nc.sync.dma_start(offsets[:], offs)
         nc.sync.dma_start(scale_pool[0:P:8, :].bitcast(I32), code_scales[0].bitcast(I32))
-        word_pool = keep.tile([P, T], U16, name="word_pool", tag="after_words", align_bytes=256)
+        word_pool = keep.tile([P, T], U16, name="word_pool", tag="after_words", align_bytes=4096)
         nc.sync.dma_start(word_pool[:].bitcast(I32), code_words[0].bitcast(I32))
         key_pools = []
         for b in range(EARLY):
-            key_pool = keep.tile([P, T], F32, name=f"key_pool{b}", align_bytes=256)
+            key_pool = keep.tile([P, T], F32, name=f"key_pool{b}", align_bytes=4096)
             nc.sync.dma_start(key_pool[:], keys[b : EARLY * P : EARLY, :])
             key_pools.append(key_pool)
 
@@ -53,9 +53,9 @@ def tile_attend_residualcache_kernel(tc, code_words, code_scales, dec, keys, off
         )
         nc.vector.tensor_copy(grouped[:, EARLY * P :, :], by_column[:, EARLY * P :, :])
 
-        spread = keep.tile([P, I], U8, name="spread", align_bytes=256)
+        spread = keep.tile([P, I], U8, name="spread", align_bytes=512)
         nc.vector.tensor_copy(spread[:], scale_pool[:].indirect(offsets[:]))
-        scales = keep.tile([P, I], U8, name="scales", align_bytes=256)
+        scales = keep.tile([P, I], U8, name="scales", align_bytes=512)
         nc.vector.tensor_copy(scales[:].bitcast(I32), spread[:].bitcast(I32))
         for r in range(1, 4):
             nc.sync.dma_start(scales[r:P:32, :].bitcast(I32), spread[8 * r : P : 32, :].bitcast(I32))
@@ -70,8 +70,8 @@ def tile_attend_residualcache_kernel(tc, code_words, code_scales, dec, keys, off
         words = shared.tile([P, I], U16, name="words", align_bytes=256, offset=4 * T)
         nc.vector.tensor_copy(words[:], word_pool[:].indirect(offsets[:]))
 
-        key_pools.append(shared.tile([P, T], F32, name="key_pool2", align_bytes=256, offset=0))
-        key_pools.append(keep.tile([P, T], F32, name="key_pool3", tag="after_words", align_bytes=256))
+        key_pools.append(shared.tile([P, T], F32, name="key_pool2", align_bytes=4096, offset=0))
+        key_pools.append(keep.tile([P, T], F32, name="key_pool3", tag="after_words", align_bytes=4096))
         for b in range(EARLY, BLOCKS):
             nc.sync.dma_start(key_pools[b][:], keys[b * P : (b + 1) * P, :])
 
@@ -102,12 +102,12 @@ def tile_attend_residualcache_kernel(tc, code_words, code_scales, dec, keys, off
             else:
                 nc.scalar.copy(sums[b][:, lo:hi], bank[:])
 
-        early_residual = keep.tile([P, EARLY, I], F32, name="early_residual", align_bytes=256)
+        early_residual = keep.tile([P, EARLY, I], F32, name="early_residual", align_bytes=4096)
         for b in range(EARLY):
             nc.vector.tensor_tensor(early_residual[:, b, :], listed[b][:], decoded[b][:], SUBTRACT)
         nc.sync.dma_start(out[: EARLY * P, :].rearrange("(p b) i -> p b i", b=EARLY), early_residual[:])
 
-        residual = keep.tile([P, I], F32, name="residual", align_bytes=256)
+        residual = keep.tile([P, I], F32, name="residual", align_bytes=4096)
         for lo in range(0, I, half):
             nc.vector.tensor_tensor(
                 residual[:, lo : lo + half],
@@ -120,7 +120,7 @@ def tile_attend_residualcache_kernel(tc, code_words, code_scales, dec, keys, off
         b = BLOCKS - 1
         first = 0
         for n, width in enumerate(LAST_PIECES):
-            piece = keep.tile([P, width], F32, name=f"piece{n}", align_bytes=256)
+            piece = keep.tile([P, width], F32, name=f"piece{n}", align_bytes=1024)
             nc.vector.tensor_tensor(
                 piece[:],
                 key_pools[b][:].indirect(offsets[:, first // 16 : (first + width) // 16]),

@@ -14,12 +14,15 @@ U8 = mybir.dt.uint8
 FP8X4 = mybir.dt.float8_e4m3fn_x4
 FP4X4 = mybir.dt.float4_e2m1fn_x4
 SUBTRACT = mybir.AluOpType.subtract
+COPY = mybir.ActivationFunctionType.Copy
 
 P = 128
 PACK = 4
 BLOCKS = D // P
-EARLY = 2
-LAST_PIECES = (256, 192, 64)
+DEALT = 2
+FUSED = 320
+LAST_FUSED = (192, 128)
+KEY_BYTES = 4 * T
 
 
 def tile_attend_residualcache_kernel(tc, code_words, code_scales, dec, keys, offs, out):
@@ -29,29 +32,24 @@ def tile_attend_residualcache_kernel(tc, code_words, code_scales, dec, keys, off
         shared = ctx.enter_context(tc.tile_pool(name="shared", bufs=1))
         psum = ctx.enter_context(tc.psum_pool(name="psum", bufs=1))
 
-        scale_pool = shared.tile([P, T], U8, name="scale_pool", align_bytes=512, offset=4 * T - T // 4)
+        def slots(lo, hi):
+            return offsets[:, lo // 16 : hi // 16]
+
+        def features(matrix, b):
+            return matrix[b : DEALT * P : DEALT, :] if b < DEALT else matrix[b * P : (b + 1) * P, :]
+
+        scale_pool = shared.tile([P, T], U8, name="scale_pool", align_bytes=512, offset=KEY_BYTES - T // 4)
         nc.vector.memset(scale_pool[:].bitcast(I32), 0)
 
-        dec_raw = keep.tile([P, PACK, D], F32, name="dec_raw", align_bytes=4096)
-        nc.sync.dma_start(dec_raw[:], dec.rearrange("(p j) d -> p j d", j=PACK))
+        word_pool = keep.tile([P, T], U16, name="word_pool", tag="after_words", align_bytes=4096)
+        nc.sync.dma_start(word_pool[:].bitcast(I32), code_words[0].bitcast(I32))
         offsets = keep.tile([P, I // 16], U16, name="offsets", align_bytes=512)
         nc.sync.dma_start(offsets[:], offs)
         nc.sync.dma_start(scale_pool[0:P:8, :].bitcast(I32), code_scales[0].bitcast(I32))
-        word_pool = keep.tile([P, T], U16, name="word_pool", tag="after_words", align_bytes=4096)
-        nc.sync.dma_start(word_pool[:].bitcast(I32), code_words[0].bitcast(I32))
-        key_pools = []
-        for b in range(EARLY):
-            key_pool = keep.tile([P, T], F32, name=f"key_pool{b}", align_bytes=4096)
-            nc.sync.dma_start(key_pool[:], keys[b : EARLY * P : EARLY, :])
-            key_pools.append(key_pool)
-
-        grouped = keep.tile([P, D, PACK], BF16, name="grouped", align_bytes=256)
-        by_column = dec_raw[:].rearrange("p j d -> p d j")
-        nc.scalar.copy(
-            grouped[:, : EARLY * P, :].rearrange("p (b m) j -> p m b j", b=EARLY),
-            by_column[:, : EARLY * P, :].rearrange("p (m b) j -> p m b j", b=EARLY),
-        )
-        nc.vector.tensor_copy(grouped[:, EARLY * P :, :], by_column[:, EARLY * P :, :])
+        dec_raw = keep.tile([P, PACK, D], F32, name="dec_raw", align_bytes=4096)
+        nc.sync.dma_start(dec_raw[:], dec.rearrange("(p j) d -> p j d", j=PACK))
+        key_pools = [keep.tile([P, T], F32, name="key_pool0", align_bytes=4096)]
+        nc.sync.dma_start(key_pools[0][:], features(keys, 0))
 
         spread = keep.tile([P, I], U8, name="spread", align_bytes=512)
         nc.vector.tensor_copy(spread[:], scale_pool[:].indirect(offsets[:]))
@@ -59,7 +57,23 @@ def tile_attend_residualcache_kernel(tc, code_words, code_scales, dec, keys, off
         nc.vector.tensor_copy(scales[:].bitcast(I32), spread[:].bitcast(I32))
         for r in range(1, 4):
             nc.sync.dma_start(scales[r:P:32, :].bitcast(I32), spread[8 * r : P : 32, :].bitcast(I32))
-        dec_codes = shared.tile([P, D], U32, name="dec_codes", align_bytes=256, offset=4 * T + 2 * I)
+        words = shared.tile([P, I], U16, name="words", align_bytes=256, offset=KEY_BYTES)
+        nc.vector.tensor_copy(words[:], word_pool[:].indirect(offsets[:]))
+
+        key_pools.append(shared.tile([P, T], F32, name="key_pool1", align_bytes=4096, offset=0))
+        key_pools.append(shared.tile([P, T], F32, name="key_pool2", align_bytes=1024, offset=KEY_BYTES + 2 * I))
+        key_pools.append(keep.tile([P, T], F32, name="key_pool3", tag="after_words", align_bytes=4096))
+        for b in range(1, BLOCKS):
+            nc.sync.dma_start(key_pools[b][:], features(keys, b))
+
+        grouped = keep.tile([P, D, PACK], BF16, name="grouped", align_bytes=256)
+        by_column = dec_raw[:].rearrange("p j d -> p d j")
+        nc.scalar.copy(
+            grouped[:, : DEALT * P, :].rearrange("p (b m) j -> p m b j", b=DEALT),
+            by_column[:, : DEALT * P, :].rearrange("p (m b) j -> p m b j", b=DEALT),
+        )
+        nc.vector.tensor_copy(grouped[:, DEALT * P :, :], by_column[:, DEALT * P :, :])
+        dec_codes = keep.tile([P, D], U32, name="dec_codes", align_bytes=256)
         dec_scales = keep.tile([P, D], U8, name="dec_scales", align_bytes=256)
         nc.vector.quantize_mx(
             out=dec_codes[:].bitcast(FP8X4),
@@ -67,65 +81,53 @@ def tile_attend_residualcache_kernel(tc, code_words, code_scales, dec, keys, off
             in_=grouped[:].rearrange("p d j -> p (d j)"),
         )
 
-        words = shared.tile([P, I], U16, name="words", align_bytes=256, offset=4 * T)
-        nc.vector.tensor_copy(words[:], word_pool[:].indirect(offsets[:]))
-
-        key_pools.append(shared.tile([P, T], F32, name="key_pool2", align_bytes=4096, offset=0))
-        key_pools.append(keep.tile([P, T], F32, name="key_pool3", tag="after_words", align_bytes=4096))
-        for b in range(EARLY, BLOCKS):
-            nc.sync.dma_start(key_pools[b][:], keys[b * P : (b + 1) * P, :])
-
-        listed = []
-        for b in range(EARLY):
-            listed_keys = keep.tile([P, I], F32, name=f"listed_keys{b}", align_bytes=256)
-            nc.vector.tensor_copy(listed_keys[:], key_pools[b][:].indirect(offsets[:]))
-            listed.append(listed_keys)
-
-        half = I // 2
-        sums = {b: keep.tile([P, I], F32, name=f"sums{b}", align_bytes=256) for b in range(EARLY, BLOCKS)}
-        passes = [(b, 0, I) for b in range(EARLY)] + [(EARLY, 0, half), (BLOCKS - 1, 0, I), (EARLY, half, I)]
-        decoded = dict(sums)
-        for b, lo, hi in passes:
+        banks = []
+        sums = []
+        for b in range(BLOCKS):
             cols = slice(b * P, (b + 1) * P)
-            bank = psum.tile([P, hi - lo], F32, name=f"bank{b}_{lo}")
+            banks.append(psum.tile([P, I], F32, name=f"bank{b}"))
             nc.tensor.matmul_mx(
-                out=bank[:],
+                out=banks[b][:],
                 lhsT=dec_codes[:, cols].bitcast(FP8X4),
                 lhsT_scale=dec_scales[:, cols],
-                rhs=words[:, lo:hi].bitcast(FP4X4),
-                rhs_scale=scales[:, lo:hi],
+                rhs=words[:].bitcast(FP4X4),
+                rhs_scale=scales[:],
                 start=True,
                 stop=True,
             )
-            if b < EARLY:
-                decoded[b] = bank
-            else:
-                nc.scalar.copy(sums[b][:, lo:hi], bank[:])
+            sums.append(keep.tile([P, FUSED], F32, name=f"sums{b}", align_bytes=256))
+            nc.scalar.copy(sums[b][:], banks[b][:, :FUSED])
 
-        early_residual = keep.tile([P, EARLY, I], F32, name="early_residual", align_bytes=4096)
-        for b in range(EARLY):
-            nc.vector.tensor_tensor(early_residual[:, b, :], listed[b][:], decoded[b][:], SUBTRACT)
-        nc.sync.dma_start(out[: EARLY * P, :].rearrange("(p b) i -> p b i", b=EARLY), early_residual[:])
+        def fused(target, b, lo, hi):
+            nc.vector.tensor_tensor(target, key_pools[b][:].indirect(slots(lo, hi)), sums[b][:, lo:hi], SUBTRACT)
 
-        residual = keep.tile([P, I], F32, name="residual", align_bytes=4096)
-        for lo in range(0, I, half):
-            nc.vector.tensor_tensor(
-                residual[:, lo : lo + half],
-                key_pools[EARLY][:].indirect(offsets[:, lo // 16 : (lo + half) // 16]),
-                decoded[EARLY][:, lo : lo + half],
-                SUBTRACT,
-            )
-        nc.sync.dma_start(out[EARLY * P : (EARLY + 1) * P, :], residual[:])
+        def picked_by_scalar(b):
+            picked = keep.tile([P, I - FUSED], F32, name=f"picked{b}", align_bytes=256)
+            nc.scalar.activation(picked[:], key_pools[b][:].indirect(slots(FUSED, I)), COPY)
+            return picked
+
+        dealt_residual = keep.tile([P, DEALT, I], F32, name="dealt_residual", align_bytes=4096)
+        for b in range(DEALT):
+            picked = picked_by_scalar(b)
+            fused(dealt_residual[:, b, :FUSED], b, 0, FUSED)
+            nc.vector.tensor_tensor(dealt_residual[:, b, FUSED:], picked[:], banks[b][:, FUSED:], SUBTRACT)
+        nc.sync.dma_start(out[: DEALT * P, :].rearrange("(p b) i -> p b i", b=DEALT), dealt_residual[:])
+
+        for b in range(DEALT, BLOCKS - 1):
+            residual = keep.tile([P, I], F32, name=f"residual{b}", align_bytes=4096)
+            picked = picked_by_scalar(b)
+            fused(residual[:, :FUSED], b, 0, FUSED)
+            nc.vector.tensor_tensor(residual[:, FUSED:], picked[:], banks[b][:, FUSED:], SUBTRACT)
+            nc.sync.dma_start(features(out, b), residual[:])
 
         b = BLOCKS - 1
+        picked = picked_by_scalar(b)
         first = 0
-        for n, width in enumerate(LAST_PIECES):
+        for n, width in enumerate(LAST_FUSED):
             piece = keep.tile([P, width], F32, name=f"piece{n}", align_bytes=1024)
-            nc.vector.tensor_tensor(
-                piece[:],
-                key_pools[b][:].indirect(offsets[:, first // 16 : (first + width) // 16]),
-                decoded[b][:, first : first + width],
-                SUBTRACT,
-            )
-            nc.sync.dma_start(out[b * P : (b + 1) * P, first : first + width], piece[:])
+            fused(piece[:], b, first, first + width)
+            nc.sync.dma_start(features(out, b)[:, first : first + width], piece[:])
             first = first + width
+        last_piece = keep.tile([P, I - FUSED], F32, name="last_piece", align_bytes=1024)
+        nc.vector.tensor_tensor(last_piece[:], picked[:], banks[b][:, FUSED:], SUBTRACT)
+        nc.sync.dma_start(features(out, b)[:, FUSED:], last_piece[:])

@@ -19,10 +19,9 @@ COPY = mybir.ActivationFunctionType.Copy
 P = 128
 PACK = 4
 BLOCKS = D // P
-DEALT = 2
 FUSED = 320
 LAST_FUSED = (192, 128)
-KEY_BYTES = 4 * T
+PAIR_BYTES = 2 * 4 * T
 
 
 def tile_attend_residualcache_kernel(tc, code_words, code_scales, dec, keys, offs, out):
@@ -35,10 +34,10 @@ def tile_attend_residualcache_kernel(tc, code_words, code_scales, dec, keys, off
         def slots(lo, hi):
             return offsets[:, lo // 16 : hi // 16]
 
-        def features(matrix, b):
-            return matrix[b : DEALT * P : DEALT, :] if b < DEALT else matrix[b * P : (b + 1) * P, :]
+        def rows(b):
+            return slice(b * P, (b + 1) * P)
 
-        scale_pool = shared.tile([P, T], U8, name="scale_pool", align_bytes=512, offset=KEY_BYTES - T // 4)
+        scale_pool = shared.tile([P, T], U8, name="scale_pool", align_bytes=512, offset=PAIR_BYTES - T // 4)
         nc.vector.memset(scale_pool[:].bitcast(I32), 0)
 
         word_pool = keep.tile([P, T], U16, name="word_pool", tag="after_words", align_bytes=4096)
@@ -48,8 +47,8 @@ def tile_attend_residualcache_kernel(tc, code_words, code_scales, dec, keys, off
         nc.sync.dma_start(scale_pool[0:P:8, :].bitcast(I32), code_scales[0].bitcast(I32))
         dec_raw = keep.tile([P, PACK, D], F32, name="dec_raw", align_bytes=4096)
         nc.sync.dma_start(dec_raw[:], dec.rearrange("(p j) d -> p j d", j=PACK))
-        key_pools = [keep.tile([P, T], F32, name="key_pool0", align_bytes=4096)]
-        nc.sync.dma_start(key_pools[0][:], features(keys, 0))
+        first_keys = keep.tile([P, T], F32, name="first_keys", align_bytes=4096)
+        nc.sync.dma_start(first_keys[:], keys[rows(0), :])
 
         spread = keep.tile([P, I], U8, name="spread", align_bytes=512)
         nc.vector.tensor_copy(spread[:], scale_pool[:].indirect(offsets[:]))
@@ -57,22 +56,21 @@ def tile_attend_residualcache_kernel(tc, code_words, code_scales, dec, keys, off
         nc.vector.tensor_copy(scales[:].bitcast(I32), spread[:].bitcast(I32))
         for r in range(1, 4):
             nc.sync.dma_start(scales[r:P:32, :].bitcast(I32), spread[8 * r : P : 32, :].bitcast(I32))
-        words = shared.tile([P, I], U16, name="words", align_bytes=256, offset=KEY_BYTES)
+        words = shared.tile([P, I], U16, name="words", align_bytes=256, offset=PAIR_BYTES)
         nc.vector.tensor_copy(words[:], word_pool[:].indirect(offsets[:]))
 
-        key_pools.append(shared.tile([P, T], F32, name="key_pool1", align_bytes=4096, offset=0))
-        key_pools.append(shared.tile([P, T], F32, name="key_pool2", align_bytes=1024, offset=KEY_BYTES + 2 * I))
-        key_pools.append(keep.tile([P, T], F32, name="key_pool3", tag="after_words", align_bytes=4096))
-        for b in range(1, BLOCKS):
-            nc.sync.dma_start(key_pools[b][:], features(keys, b))
+        pair_keys = shared.tile([P, 2 * T], F32, name="pair_keys", align_bytes=4096, offset=0)
+        nc.sync.dma_start(
+            pair_keys[:].rearrange("p (b t) -> p b t", b=2),
+            keys[P : 3 * P, :].rearrange("(b p) t -> p b t", b=2),
+        )
+        last_keys = keep.tile([P, T], F32, name="last_keys", tag="after_words", align_bytes=4096)
+        nc.sync.dma_start(last_keys[:], keys[rows(BLOCKS - 1), :])
 
         grouped = keep.tile([P, D, PACK], BF16, name="grouped", align_bytes=256)
         by_column = dec_raw[:].rearrange("p j d -> p d j")
-        nc.scalar.copy(
-            grouped[:, : DEALT * P, :].rearrange("p (b m) j -> p m b j", b=DEALT),
-            by_column[:, : DEALT * P, :].rearrange("p (m b) j -> p m b j", b=DEALT),
-        )
-        nc.vector.tensor_copy(grouped[:, DEALT * P :, :], by_column[:, DEALT * P :, :])
+        nc.scalar.copy(grouped[:, : D // 2, :], by_column[:, : D // 2, :])
+        nc.vector.tensor_copy(grouped[:, D // 2 :, :], by_column[:, D // 2 :, :])
         dec_codes = keep.tile([P, D], U32, name="dec_codes", align_bytes=256)
         dec_scales = keep.tile([P, D], U8, name="dec_scales", align_bytes=256)
         nc.vector.quantize_mx(
@@ -81,53 +79,51 @@ def tile_attend_residualcache_kernel(tc, code_words, code_scales, dec, keys, off
             in_=grouped[:].rearrange("p d j -> p (d j)"),
         )
 
+        first_listed = keep.tile([P, I], F32, name="first_listed", align_bytes=256)
+        nc.scalar.activation(first_listed[:], first_keys[:].indirect(offsets[:]), COPY)
+
         banks = []
-        sums = []
         for b in range(BLOCKS):
-            cols = slice(b * P, (b + 1) * P)
             banks.append(psum.tile([P, I], F32, name=f"bank{b}"))
             nc.tensor.matmul_mx(
                 out=banks[b][:],
-                lhsT=dec_codes[:, cols].bitcast(FP8X4),
-                lhsT_scale=dec_scales[:, cols],
+                lhsT=dec_codes[:, rows(b)].bitcast(FP8X4),
+                lhsT_scale=dec_scales[:, rows(b)],
                 rhs=words[:].bitcast(FP4X4),
                 rhs_scale=scales[:],
                 start=True,
                 stop=True,
             )
-            sums.append(keep.tile([P, FUSED], F32, name=f"sums{b}", align_bytes=256))
-            nc.scalar.copy(sums[b][:], banks[b][:, :FUSED])
+        pair_sums = keep.tile([P, I], F32, name="pair_sums", align_bytes=256)
+        nc.scalar.copy(pair_sums[:], banks[1][:])
+        last_sums = keep.tile([P, FUSED], F32, name="last_sums", align_bytes=256)
+        nc.scalar.copy(last_sums[:], banks[BLOCKS - 1][:, :FUSED])
 
-        def fused(target, b, lo, hi):
-            nc.vector.tensor_tensor(target, key_pools[b][:].indirect(slots(lo, hi)), sums[b][:, lo:hi], SUBTRACT)
+        residuals = [keep.tile([P, I], F32, name=f"residual{b}", align_bytes=4096) for b in range(BLOCKS - 1)]
+        nc.vector.tensor_tensor(residuals[0][:], first_listed[:], banks[0][:], SUBTRACT)
+        nc.sync.dma_start(out[rows(0), :], residuals[0][:])
 
-        def picked_by_scalar(b):
-            picked = keep.tile([P, I - FUSED], F32, name=f"picked{b}", align_bytes=256)
-            nc.scalar.activation(picked[:], key_pools[b][:].indirect(slots(FUSED, I)), COPY)
-            return picked
-
-        dealt_residual = keep.tile([P, DEALT, I], F32, name="dealt_residual", align_bytes=4096)
-        for b in range(DEALT):
-            picked = picked_by_scalar(b)
-            fused(dealt_residual[:, b, :FUSED], b, 0, FUSED)
-            nc.vector.tensor_tensor(dealt_residual[:, b, FUSED:], picked[:], banks[b][:, FUSED:], SUBTRACT)
-        nc.sync.dma_start(out[: DEALT * P, :].rearrange("(p b) i -> p b i", b=DEALT), dealt_residual[:])
-
-        for b in range(DEALT, BLOCKS - 1):
-            residual = keep.tile([P, I], F32, name=f"residual{b}", align_bytes=4096)
-            picked = picked_by_scalar(b)
-            fused(residual[:, :FUSED], b, 0, FUSED)
-            nc.vector.tensor_tensor(residual[:, FUSED:], picked[:], banks[b][:, FUSED:], SUBTRACT)
-            nc.sync.dma_start(features(out, b), residual[:])
+        pair_listed = keep.tile([P, I], F32, name="pair_listed", align_bytes=256)
+        nc.scalar.activation(pair_listed[:], pair_keys[:, T:].indirect(offsets[:]), COPY)
+        nc.vector.tensor_tensor(residuals[1][:], pair_keys[:].indirect(offsets[:]), pair_sums[:], SUBTRACT)
+        nc.sync.dma_start(out[rows(1), :], residuals[1][:])
+        nc.vector.tensor_tensor(residuals[2][:], pair_listed[:], banks[2][:], SUBTRACT)
+        nc.sync.dma_start(out[rows(2), :], residuals[2][:])
 
         b = BLOCKS - 1
-        picked = picked_by_scalar(b)
+        last_listed = keep.tile([P, I - FUSED], F32, name="last_listed", align_bytes=256)
+        nc.scalar.activation(last_listed[:], last_keys[:].indirect(slots(FUSED, I)), COPY)
         first = 0
         for n, width in enumerate(LAST_FUSED):
             piece = keep.tile([P, width], F32, name=f"piece{n}", align_bytes=1024)
-            fused(piece[:], b, first, first + width)
-            nc.sync.dma_start(features(out, b)[:, first : first + width], piece[:])
+            nc.vector.tensor_tensor(
+                piece[:],
+                last_keys[:].indirect(slots(first, first + width)),
+                last_sums[:, first : first + width],
+                SUBTRACT,
+            )
+            nc.sync.dma_start(out[rows(b), first : first + width], piece[:])
             first = first + width
         last_piece = keep.tile([P, I - FUSED], F32, name="last_piece", align_bytes=1024)
-        nc.vector.tensor_tensor(last_piece[:], picked[:], banks[b][:, FUSED:], SUBTRACT)
-        nc.sync.dma_start(features(out, b)[:, FUSED:], last_piece[:])
+        nc.vector.tensor_tensor(last_piece[:], last_listed[:], banks[b][:, FUSED:], SUBTRACT)
+        nc.sync.dma_start(out[rows(b), FUSED:], last_piece[:])

@@ -104,10 +104,13 @@ def tile_attend_residualcache_kernel(tc, code_words, code_scales, dec, keys, off
         nc.sync.dma_start(out[rows(0), :], residuals[0][:])
 
         pair_listed = keep.tile([P, I], F32, name="pair_listed", align_bytes=256)
-        nc.scalar.activation(pair_listed[:], pair_keys[:, T:].indirect(offsets[:]), COPY)
+        halves = [(lo, lo + I // 2) for lo in range(0, I, I // 2)]
+        for lo, hi in halves:
+            nc.scalar.activation(pair_listed[:, lo:hi], pair_keys[:, T:].indirect(slots(lo, hi)), COPY)
         nc.vector.tensor_tensor(residuals[1][:], pair_keys[:].indirect(offsets[:]), pair_sums[:], SUBTRACT)
         nc.sync.dma_start(out[rows(1), :], residuals[1][:])
-        nc.vector.tensor_tensor(residuals[2][:], pair_listed[:], banks[2][:], SUBTRACT)
+        for lo, hi in halves:
+            nc.vector.tensor_tensor(residuals[2][:, lo:hi], pair_listed[:, lo:hi], banks[2][:, lo:hi], SUBTRACT)
         nc.sync.dma_start(out[rows(2), :], residuals[2][:])
 
         b = BLOCKS - 1

@@ -21,7 +21,7 @@ PACK = 4
 BLOCKS = D // P
 FUSED = 320
 LAST_FUSED = (192, 128)
-PAIR_BYTES = 2 * 4 * T
+POOL_BYTES = 4 * T
 
 
 def tile_attend_residualcache_kernel(tc, code_words, code_scales, dec, keys, offs, out):
@@ -37,7 +37,7 @@ def tile_attend_residualcache_kernel(tc, code_words, code_scales, dec, keys, off
         def rows(b):
             return slice(b * P, (b + 1) * P)
 
-        scale_pool = shared.tile([P, T], U8, name="scale_pool", align_bytes=512, offset=PAIR_BYTES - T // 4)
+        scale_pool = shared.tile([P, T], U8, name="scale_pool", align_bytes=512, offset=POOL_BYTES - T // 4)
         nc.vector.memset(scale_pool[:].bitcast(I32), 0)
 
         word_pool = keep.tile([P, T], U16, name="word_pool", tag="after_words", align_bytes=4096)
@@ -47,8 +47,11 @@ def tile_attend_residualcache_kernel(tc, code_words, code_scales, dec, keys, off
         nc.sync.dma_start(scale_pool[0:P:8, :].bitcast(I32), code_scales[0].bitcast(I32))
         dec_raw = keep.tile([P, PACK, D], F32, name="dec_raw", align_bytes=4096)
         nc.sync.dma_start(dec_raw[:], dec.rearrange("(p j) d -> p j d", j=PACK))
-        first_keys = keep.tile([P, T], F32, name="first_keys", align_bytes=4096)
-        nc.sync.dma_start(first_keys[:], keys[rows(0), :])
+        pair_keys = keep.tile([P, 2 * T], F32, name="pair_keys", align_bytes=4096)
+        nc.sync.dma_start(
+            pair_keys[:].rearrange("p (b t) -> p b t", b=2),
+            keys[0 : 2 * P, :].rearrange("(b p) t -> p b t", b=2),
+        )
 
         spread = keep.tile([P, I], U8, name="spread", align_bytes=512)
         nc.vector.tensor_copy(spread[:], scale_pool[:].indirect(offsets[:]))
@@ -56,18 +59,15 @@ def tile_attend_residualcache_kernel(tc, code_words, code_scales, dec, keys, off
         nc.vector.tensor_copy(scales[:].bitcast(I32), spread[:].bitcast(I32))
         for r in range(1, 4):
             nc.sync.dma_start(scales[r:P:32, :].bitcast(I32), spread[8 * r : P : 32, :].bitcast(I32))
-        words = shared.tile([P, I], U16, name="words", align_bytes=256, offset=PAIR_BYTES)
+        words = shared.tile([P, I], U16, name="words", align_bytes=256, offset=POOL_BYTES)
         nc.vector.tensor_copy(words[:], word_pool[:].indirect(offsets[:]))
 
-        pair_keys = shared.tile([P, 2 * T], F32, name="pair_keys", align_bytes=4096, offset=0)
-        nc.sync.dma_start(
-            pair_keys[:].rearrange("p (b t) -> p b t", b=2),
-            keys[P : 3 * P, :].rearrange("(b p) t -> p b t", b=2),
-        )
+        third_keys = shared.tile([P, T], F32, name="third_keys", align_bytes=4096, offset=0)
+        nc.sync.dma_start(third_keys[:], keys[rows(2), :])
         last_keys = keep.tile([P, T], F32, name="last_keys", tag="after_words", align_bytes=4096)
-        nc.sync.dma_start(last_keys[:], keys[rows(BLOCKS - 1), :])
+        nc.sync.dma_start(last_keys[:], keys[rows(3), :])
 
-        grouped = keep.tile([P, D, PACK], BF16, name="grouped", align_bytes=256)
+        grouped = keep.tile([P, D, PACK], BF16, name="grouped", tag="quantiser_input", align_bytes=256)
         by_column = dec_raw[:].rearrange("p j d -> p d j")
         nc.scalar.copy(grouped[:, : D // 2, :], by_column[:, : D // 2, :])
         nc.vector.tensor_copy(grouped[:, D // 2 :, :], by_column[:, D // 2 :, :])
@@ -80,7 +80,9 @@ def tile_attend_residualcache_kernel(tc, code_words, code_scales, dec, keys, off
         )
 
         first_listed = keep.tile([P, I], F32, name="first_listed", align_bytes=256)
-        nc.scalar.activation(first_listed[:], first_keys[:].indirect(offsets[:]), COPY)
+        nc.scalar.activation(first_listed[:], pair_keys[:, :T].indirect(offsets[:]), COPY)
+        second_listed = keep.tile([P, I], F32, name="second_listed", tag="quantiser_input", align_bytes=256)
+        nc.vector.tensor_copy(second_listed[:], pair_keys[:, T:].indirect(offsets[:]))
 
         banks = []
         for b in range(BLOCKS):
@@ -94,24 +96,23 @@ def tile_attend_residualcache_kernel(tc, code_words, code_scales, dec, keys, off
                 start=True,
                 stop=True,
             )
-        pair_sums = keep.tile([P, I], F32, name="pair_sums", align_bytes=256)
-        nc.scalar.copy(pair_sums[:], banks[1][:])
+
+        for b, listed in enumerate((first_listed, second_listed)):
+            residual = keep.tile([P, I], F32, name=f"residual{b}", align_bytes=4096)
+            nc.vector.tensor_tensor(residual[:], listed[:], banks[b][:], SUBTRACT)
+            nc.sync.dma_start(out[rows(b), :], residual[:])
+
+        third_sums = keep.tile([P, FUSED], F32, name="third_sums", align_bytes=256)
+        nc.scalar.copy(third_sums[:], banks[2][:, :FUSED])
         last_sums = keep.tile([P, FUSED], F32, name="last_sums", align_bytes=256)
-        nc.scalar.copy(last_sums[:], banks[BLOCKS - 1][:, :FUSED])
+        nc.scalar.copy(last_sums[:], banks[3][:, :FUSED])
 
-        residuals = [keep.tile([P, I], F32, name=f"residual{b}", align_bytes=4096) for b in range(BLOCKS - 1)]
-        nc.vector.tensor_tensor(residuals[0][:], first_listed[:], banks[0][:], SUBTRACT)
-        nc.sync.dma_start(out[rows(0), :], residuals[0][:])
-
-        pair_listed = keep.tile([P, I], F32, name="pair_listed", align_bytes=256)
-        halves = [(lo, lo + I // 2) for lo in range(0, I, I // 2)]
-        for lo, hi in halves:
-            nc.scalar.activation(pair_listed[:, lo:hi], pair_keys[:, T:].indirect(slots(lo, hi)), COPY)
-        nc.vector.tensor_tensor(residuals[1][:], pair_keys[:].indirect(offsets[:]), pair_sums[:], SUBTRACT)
-        nc.sync.dma_start(out[rows(1), :], residuals[1][:])
-        for lo, hi in halves:
-            nc.vector.tensor_tensor(residuals[2][:, lo:hi], pair_listed[:, lo:hi], banks[2][:, lo:hi], SUBTRACT)
-        nc.sync.dma_start(out[rows(2), :], residuals[2][:])
+        third_listed = keep.tile([P, I - FUSED], F32, name="third_listed", align_bytes=256)
+        nc.scalar.activation(third_listed[:], third_keys[:].indirect(slots(FUSED, I)), COPY)
+        third = keep.tile([P, I], F32, name="third", align_bytes=4096)
+        nc.vector.tensor_tensor(third[:, :FUSED], third_keys[:].indirect(slots(0, FUSED)), third_sums[:], SUBTRACT)
+        nc.vector.tensor_tensor(third[:, FUSED:], third_listed[:], banks[2][:, FUSED:], SUBTRACT)
+        nc.sync.dma_start(out[rows(2), :], third[:])
 
         b = BLOCKS - 1
         last_listed = keep.tile([P, I - FUSED], F32, name="last_listed", align_bytes=256)

@@ -40,7 +40,7 @@ def tile_attend_residualcache_kernel(tc, code_words, code_scales, dec, keys, off
         scale_pool = shared.tile([P, T], U8, name="scale_pool", align_bytes=512, offset=POOL_BYTES - T // 4)
         nc.vector.memset(scale_pool[:].bitcast(I32), 0)
 
-        word_pool = keep.tile([P, T], U16, name="word_pool", tag="after_words", align_bytes=4096)
+        word_pool = keep.tile([P, T], U16, name="word_pool", align_bytes=4096)
         nc.sync.dma_start(word_pool[:].bitcast(I32), code_words[0].bitcast(I32))
         offsets = keep.tile([P, I // 16], U16, name="offsets", align_bytes=512)
         nc.sync.dma_start(offsets[:], offs)
@@ -53,7 +53,7 @@ def tile_attend_residualcache_kernel(tc, code_words, code_scales, dec, keys, off
             keys[0 : 2 * P, :].rearrange("(b p) t -> p b t", b=2),
         )
 
-        spread = keep.tile([P, I], U8, name="spread", align_bytes=512)
+        spread = keep.tile([P, I], U8, name="spread", tag="after_moves", align_bytes=4096)
         nc.vector.tensor_copy(spread[:], scale_pool[:].indirect(offsets[:]))
         scales = keep.tile([P, I], U8, name="scales", align_bytes=512)
         nc.vector.tensor_copy(scales[:].bitcast(I32), spread[:].bitcast(I32))
@@ -64,7 +64,7 @@ def tile_attend_residualcache_kernel(tc, code_words, code_scales, dec, keys, off
 
         third_keys = shared.tile([P, T], F32, name="third_keys", align_bytes=4096, offset=0)
         nc.sync.dma_start(third_keys[:], keys[rows(2), :])
-        last_keys = keep.tile([P, T], F32, name="last_keys", tag="after_words", align_bytes=4096)
+        last_keys = keep.tile([P, T], F32, name="last_keys", tag="after_moves", align_bytes=4096)
         nc.sync.dma_start(last_keys[:], keys[rows(3), :])
 
         grouped = keep.tile([P, D, PACK], BF16, name="grouped", tag="quantiser_input", align_bytes=256)
@@ -84,9 +84,8 @@ def tile_attend_residualcache_kernel(tc, code_words, code_scales, dec, keys, off
         second_listed = keep.tile([P, I], F32, name="second_listed", tag="quantiser_input", align_bytes=256)
         nc.vector.tensor_copy(second_listed[:], pair_keys[:, T:].indirect(offsets[:]))
 
-        banks = []
-        for b in range(BLOCKS):
-            banks.append(psum.tile([P, I], F32, name=f"bank{b}"))
+        banks = [psum.tile([P, I], F32, name=f"bank{b}") for b in range(BLOCKS)]
+        for b in (0, 2, 3, 1):
             nc.tensor.matmul_mx(
                 out=banks[b][:],
                 lhsT=dec_codes[:, rows(b)].bitcast(FP8X4),

@@ -48,10 +48,7 @@ def tile_attend_residualcache_kernel(tc, code_words, code_scales, dec, keys, off
         dec_raw = keep.tile([P, PACK, D], F32, name="dec_raw", align_bytes=4096)
         nc.sync.dma_start(dec_raw[:], dec.rearrange("(p j) d -> p j d", j=PACK))
         pair_keys = keep.tile([P, 2 * T], F32, name="pair_keys", align_bytes=4096)
-        nc.sync.dma_start(
-            pair_keys[:].rearrange("p (b t) -> p b t", b=2),
-            keys[0 : 2 * P, :].rearrange("(b p) t -> p b t", b=2),
-        )
+        nc.sync.dma_start(pair_keys[:], keys[0 : 2 * P, :].rearrange("(p b) t -> p (b t)", b=2))
 
         spread = keep.tile([P, I], U8, name="spread", tag="after_moves", align_bytes=4096)
         nc.vector.tensor_copy(spread[:], scale_pool[:].indirect(offsets[:]))
@@ -69,7 +66,10 @@ def tile_attend_residualcache_kernel(tc, code_words, code_scales, dec, keys, off
 
         grouped = keep.tile([P, D, PACK], BF16, name="grouped", tag="quantiser_input", align_bytes=256)
         by_column = dec_raw[:].rearrange("p j d -> p d j")
-        nc.scalar.copy(grouped[:, : D // 2, :], by_column[:, : D // 2, :])
+        nc.scalar.copy(
+            grouped[:, : D // 2, :].rearrange("p (b m) j -> p b m j", b=2),
+            by_column[:, : D // 2, :].rearrange("p (m b) j -> p b m j", b=2),
+        )
         nc.vector.tensor_copy(grouped[:, D // 2 :, :], by_column[:, D // 2 :, :])
         dec_codes = keep.tile([P, D], U32, name="dec_codes", align_bytes=256)
         dec_scales = keep.tile([P, D], U8, name="dec_scales", align_bytes=256)
@@ -99,7 +99,7 @@ def tile_attend_residualcache_kernel(tc, code_words, code_scales, dec, keys, off
         for b, listed in enumerate((first_listed, second_listed)):
             residual = keep.tile([P, I], F32, name=f"residual{b}", align_bytes=4096)
             nc.vector.tensor_tensor(residual[:], listed[:], banks[b][:], SUBTRACT)
-            nc.sync.dma_start(out[rows(b), :], residual[:])
+            nc.sync.dma_start(out[b : 2 * P : 2, :], residual[:])
 
         third_sums = keep.tile([P, FUSED], F32, name="third_sums", align_bytes=256)
         nc.scalar.copy(third_sums[:], banks[2][:, :FUSED])

@@ -19,6 +19,7 @@ COPY = mybir.ActivationFunctionType.Copy
 P = 128
 PACK = 4
 BLOCKS = D // P
+HALF = I // 2
 FUSED = 320
 LAST_FUSED = (192, 128)
 POOL_BYTES = 4 * T
@@ -84,33 +85,44 @@ def tile_attend_residualcache_kernel(tc, code_words, code_scales, dec, keys, off
         second_listed = keep.tile([P, I], F32, name="second_listed", tag="quantiser_input", align_bytes=256)
         nc.vector.tensor_copy(second_listed[:], pair_keys[:, T:].indirect(offsets[:]))
 
-        banks = [psum.tile([P, I], F32, name=f"bank{b}") for b in range(BLOCKS)]
-        for b in (0, 2, 3, 1):
+        def product(target, b, lo, hi):
             nc.tensor.matmul_mx(
-                out=banks[b][:],
+                out=target,
                 lhsT=dec_codes[:, rows(b)].bitcast(FP8X4),
                 lhsT_scale=dec_scales[:, rows(b)],
-                rhs=words[:].bitcast(FP4X4),
-                rhs_scale=scales[:],
+                rhs=words[:, lo:hi].bitcast(FP4X4),
+                rhs_scale=scales[:, lo:hi],
                 start=True,
                 stop=True,
             )
 
+        pair_banks = [psum.tile([P, I], F32, name=f"pair_bank{b}") for b in range(2)]
+        third_low = psum.tile([P, HALF], F32, name="third_low")
+        last_high = psum.tile([P, HALF], F32, name="last_high")
+        mixed = psum.tile([P, I], F32, name="mixed")
+        product(pair_banks[0][:], 0, 0, I)
+        product(third_low[:], 2, 0, HALF)
+        product(pair_banks[1][:], 1, 0, I)
+        product(last_high[:], 3, HALF, I)
+        product(mixed[:, :HALF], 3, 0, HALF)
+
         for b, listed in enumerate((first_listed, second_listed)):
             residual = keep.tile([P, I], F32, name=f"residual{b}", align_bytes=4096)
-            nc.vector.tensor_tensor(residual[:], listed[:], banks[b][:], SUBTRACT)
+            nc.vector.tensor_tensor(residual[:], listed[:], pair_banks[b][:], SUBTRACT)
             nc.sync.dma_start(out[b : 2 * P : 2, :], residual[:])
 
-        third_sums = keep.tile([P, FUSED], F32, name="third_sums", align_bytes=256)
-        nc.scalar.copy(third_sums[:], banks[2][:, :FUSED])
+        third_sums = keep.tile([P, HALF], F32, name="third_sums", align_bytes=256)
+        nc.scalar.copy(third_sums[:], third_low[:])
+        third_listed = keep.tile([P, HALF], F32, name="third_listed", align_bytes=256)
+        nc.scalar.activation(third_listed[:], third_keys[:].indirect(slots(HALF, I)), COPY)
         last_sums = keep.tile([P, FUSED], F32, name="last_sums", align_bytes=256)
-        nc.scalar.copy(last_sums[:], banks[3][:, :FUSED])
+        nc.scalar.copy(last_sums[:, HALF:], last_high[:, : FUSED - HALF])
+        nc.scalar.copy(last_sums[:, :HALF], mixed[:, :HALF])
+        product(mixed[:, HALF:], 2, HALF, I)
 
-        third_listed = keep.tile([P, I - FUSED], F32, name="third_listed", align_bytes=256)
-        nc.scalar.activation(third_listed[:], third_keys[:].indirect(slots(FUSED, I)), COPY)
         third = keep.tile([P, I], F32, name="third", align_bytes=4096)
-        nc.vector.tensor_tensor(third[:, :FUSED], third_keys[:].indirect(slots(0, FUSED)), third_sums[:], SUBTRACT)
-        nc.vector.tensor_tensor(third[:, FUSED:], third_listed[:], banks[2][:, FUSED:], SUBTRACT)
+        nc.vector.tensor_tensor(third[:, :HALF], third_keys[:].indirect(slots(0, HALF)), third_sums[:], SUBTRACT)
+        nc.vector.tensor_tensor(third[:, HALF:], third_listed[:], mixed[:, HALF:], SUBTRACT)
         nc.sync.dma_start(out[rows(2), :], third[:])
 
         b = BLOCKS - 1
@@ -128,5 +140,5 @@ def tile_attend_residualcache_kernel(tc, code_words, code_scales, dec, keys, off
             nc.sync.dma_start(out[rows(b), first : first + width], piece[:])
             first = first + width
         last_piece = keep.tile([P, I - FUSED], F32, name="last_piece", align_bytes=1024)
-        nc.vector.tensor_tensor(last_piece[:], last_listed[:], banks[b][:, FUSED:], SUBTRACT)
+        nc.vector.tensor_tensor(last_piece[:], last_listed[:], last_high[:, FUSED - HALF :], SUBTRACT)
         nc.sync.dma_start(out[rows(b), FUSED:], last_piece[:])

from contextlib import ExitStack

import concourse.mybir as mybir

C, T, I, D = 512, 2048, 512, 512
FLOPS = 2 * C * I * D

F32 = mybir.dt.float32
BF16 = mybir.dt.bfloat16
I32 = mybir.dt.int32
U32 = mybir.dt.uint32
U16 = mybir.dt.uint16
U8 = mybir.dt.uint8
FP8X4 = mybir.dt.float8_e4m3fn_x4
FP4X4 = mybir.dt.float4_e2m1fn_x4
SUBTRACT = mybir.AluOpType.subtract
COPY = mybir.ActivationFunctionType.Copy

P = 128
PACK = 4
BLOCKS = D // P
HALF = I // 2
FUSED = 320
LAST_FUSED = (192, 128)
POOL_BYTES = 4 * T


def tile_attend_residualcache_kernel(tc, code_words, code_scales, dec, keys, offs, out):
    nc = tc.nc
    with ExitStack() as ctx:
        keep = ctx.enter_context(tc.tile_pool(name="keep", bufs=1))
        shared = ctx.enter_context(tc.tile_pool(name="shared", bufs=1))
        psum = ctx.enter_context(tc.psum_pool(name="psum", bufs=1))

        def slots(lo, hi):
            return offsets[:, lo // 16 : hi // 16]

        def rows(b):
            return slice(b * P, (b + 1) * P)

        scale_pool = shared.tile([P, T], U8, name="scale_pool", align_bytes=512, offset=POOL_BYTES - T // 4)
        nc.vector.memset(scale_pool[:].bitcast(I32), 0)

        word_pool = keep.tile([P, T], U16, name="word_pool", align_bytes=4096)
        nc.sync.dma_start(word_pool[:].bitcast(I32), code_words[0].bitcast(I32))
        offsets = keep.tile([P, I // 16], U16, name="offsets", align_bytes=512)
        nc.sync.dma_start(offsets[:], offs)
        nc.sync.dma_start(scale_pool[0:P:8, :].bitcast(I32), code_scales[0].bitcast(I32))
        dec_raw = keep.tile([P, PACK, D], F32, name="dec_raw", align_bytes=4096)
        nc.sync.dma_start(dec_raw[:], dec.rearrange("(p j) d -> p j d", j=PACK))
        pair_keys = keep.tile([P, 2 * T], F32, name="pair_keys", align_bytes=4096)
        nc.sync.dma_start(pair_keys[:], keys[0 : 2 * P, :].rearrange("(p b) t -> p (b t)", b=2))

        spread = keep.tile([P, I], U8, name="spread", tag="after_moves", align_bytes=4096)
        nc.vector.tensor_copy(spread[:], scale_pool[:].indirect(offsets[:]))
        scales = keep.tile([P, I], U8, name="scales", align_bytes=512)
        nc.vector.tensor_copy(scales[:].bitcast(I32), spread[:].bitcast(I32))
        for r in range(1, 4):
            nc.sync.dma_start(scales[r:P:32, :].bitcast(I32), spread[8 * r : P : 32, :].bitcast(I32))
        words = shared.tile([P, I], U16, name="words", align_bytes=256, offset=POOL_BYTES)
        nc.vector.tensor_copy(words[:], word_pool[:].indirect(offsets[:]))

        third_keys = shared.tile([P, T], F32, name="third_keys", align_bytes=4096, offset=0)
        nc.sync.dma_start(third_keys[:], keys[rows(2), :])
        last_keys = keep.tile([P, T], F32, name="last_keys", tag="after_moves", align_bytes=4096)
        nc.sync.dma_start(last_keys[:], keys[rows(3), :])

        grouped = keep.tile([P, D, PACK], BF16, name="grouped", tag="quantiser_input", align_bytes=256)
        by_column = dec_raw[:].rearrange("p j d -> p d j")
        nc.scalar.copy(
            grouped[:, : D // 2, :].rearrange("p (b m) j -> p b m j", b=2),
            by_column[:, : D // 2, :].rearrange("p (m b) j -> p b m j", b=2),
        )
        nc.vector.tensor_copy(grouped[:, D // 2 :, :], by_column[:, D // 2 :, :])
        dec_codes = keep.tile([P, D], U32, name="dec_codes", align_bytes=256)
        dec_scales = keep.tile([P, D], U8, name="dec_scales", align_bytes=256)
        nc.vector.quantize_mx(
            out=dec_codes[:].bitcast(FP8X4),
            scales=dec_scales[:],
            in_=grouped[:].rearrange("p d j -> p (d j)"),
        )

        first_listed = keep.tile([P, I], F32, name="first_listed", align_bytes=256)
        nc.scalar.activation(first_listed[:], pair_keys[:, :T].indirect(offsets[:]), COPY)
        second_listed = keep.tile([P, I], F32, name="second_listed", tag="quantiser_input", align_bytes=256)
        nc.vector.tensor_copy(second_listed[:], pair_keys[:, T:].indirect(offsets[:]))

        def product(target, b, lo, hi):
            nc.tensor.matmul_mx(
                out=target,
                lhsT=dec_codes[:, rows(b)].bitcast(FP8X4),
                lhsT_scale=dec_scales[:, rows(b)],
                rhs=words[:, lo:hi].bitcast(FP4X4),
                rhs_scale=scales[:, lo:hi],
                start=True,
                stop=True,
            )

        pair_banks = [psum.tile([P, I], F32, name=f"pair_bank{b}") for b in range(2)]
        third_low = psum.tile([P, HALF], F32, name="third_low")
        last_high = psum.tile([P, HALF], F32, name="last_high")
        mixed = psum.tile([P, I], F32, name="mixed")
        product(pair_banks[0][:], 0, 0, I)
        product(third_low[:], 2, 0, HALF)
        product(pair_banks[1][:], 1, 0, I)
        product(last_high[:], 3, HALF, I)
        product(mixed[:, :HALF], 3, 0, HALF)

        for b, listed in enumerate((first_listed, second_listed)):
            residual = keep.tile([P, I], F32, name=f"residual{b}", align_bytes=4096)
            nc.vector.tensor_tensor(residual[:], listed[:], pair_banks[b][:], SUBTRACT)
            nc.sync.dma_start(out[b : 2 * P : 2, :], residual[:])

        third_sums = keep.tile([P, HALF], F32, name="third_sums", align_bytes=256)
        nc.scalar.copy(third_sums[:], third_low[:])
        third_listed = keep.tile([P, HALF], F32, name="third_listed", align_bytes=256)
        nc.scalar.activation(third_listed[:], third_keys[:].indirect(slots(HALF, I)), COPY)
        last_sums = keep.tile([P, FUSED], F32, name="last_sums", align_bytes=256)
        nc.scalar.copy(last_sums[:, HALF:], last_high[:, : FUSED - HALF])
        nc.scalar.copy(last_sums[:, :HALF], mixed[:, :HALF])
        product(mixed[:, HALF:], 2, HALF, I)

        third = keep.tile([P, I], F32, name="third", align_bytes=4096)
        nc.vector.tensor_tensor(third[:, :HALF], third_keys[:].indirect(slots(0, HALF)), third_sums[:], SUBTRACT)
        nc.vector.tensor_tensor(third[:, HALF:], third_listed[:], mixed[:, HALF:], SUBTRACT)
        nc.sync.dma_start(out[rows(2), :], third[:])

        b = BLOCKS - 1
        last_listed = keep.tile([P, I - FUSED], F32, name="last_listed", align_bytes=256)
        nc.scalar.activation(last_listed[:], last_keys[:].indirect(slots(FUSED, I)), COPY)
        first = 0
        for n, width in enumerate(LAST_FUSED):
            piece = keep.tile([P, width], F32, name=f"piece{n}", align_bytes=1024)
            nc.vector.tensor_tensor(
                piece[:],
                last_keys[:].indirect(slots(first, first + width)),
                last_sums[:, first : first + width],
                SUBTRACT,
            )
            nc.sync.dma_start(out[rows(b), first : first + width], piece[:])
            first = first + width
        last_piece = keep.tile([P, I - FUSED], F32, name="last_piece", align_bytes=1024)
        nc.vector.tensor_tensor(last_piece[:], last_listed[:], last_high[:, FUSED - HALF :], SUBTRACT)
        nc.sync.dma_start(out[rows(b), FUSED:], last_piece[:])
